import numpy as np
import ml_dtypes


def mxq(x, axis, fmt="e4m3"):
    dtype, down = {"e4m3": (ml_dtypes.float8_e4m3fn, 7), "e5m2": (ml_dtypes.float8_e5m2, 14)}[fmt]
    v = np.moveaxis(np.asarray(x, np.float32).astype(ml_dtypes.bfloat16).astype(np.float64), axis, -1)
    blocks = v.reshape(v.shape[:-1] + (-1, 32))
    amax = np.abs(blocks).max(-1, keepdims=True)
    byte = np.maximum(np.where(amax > 0, np.frexp(amax)[1] - 1 + 127, 0) - down, 1)
    scale = np.exp2(byte - 127.0)
    codes = (blocks / scale).astype(np.float32).astype(dtype).astype(np.float64)
    return np.moveaxis((codes * scale).reshape(v.shape), -1, axis)


WIDE = False


def mx_kscale(k, group=512):
    if not WIDE:
        return np.ones(k)
    levels = np.array([18, -18])
    if group != 512:
        return np.exp2(np.random.permutation(np.resize(levels, k // group))).repeat(group)
    if k % 512:
        return np.exp2(np.random.permutation(np.resize(levels, k // 32))).repeat(32)
    a = np.empty((k // 512, 16))
    for p in range(k // 512):
        a[p, :8] = np.random.permutation(np.resize(levels, 8))
        for g in range(8):
            far = levels[np.abs(levels - a[p, g]) >= 10]
            a[p, g + 8] = far[np.random.randint(len(far))]
    return np.exp2(a.ravel()).repeat(32)


def f64(x):
    return np.asarray(x).astype(np.float64)


def sigmoid(v):
    return 1.0 / (1.0 + np.exp(-v))


G, D, I, N, J = 4, 128, 128, 512, 128


def sgn(shape):
    return np.random.uniform(0.5, 2.0, shape) * np.where(np.random.standard_normal(shape) < 0, -1.0, 1.0)


def setup_inputs():
    n = np.random.standard_normal
    s_d = mx_kscale(D, 0)
    s_i = mx_kscale(I, 0)
    return {
        "x": (n((G, D, I)) * s_d[:, None]).astype(np.float32),
        "w": (n((D, N)) / np.sqrt(D) / s_d[:, None]).astype(np.float32),
        "ni": (sgn((G, I, 1)) * s_i[:, None]).astype(np.float32),
        "ad": ((np.random.uniform(size=(G, I, J)) < 0.1) * np.random.uniform(0.5, 1.0, (G, I, J)) / 3 / s_i[:, None]).astype(np.float32),
        "og": (n((G, J, N))).astype(np.float32),
        "r": (n((G, J, N))).astype(np.float32),
    }


def reference(x, w, ni, ad, og, r):
    xq = mxq(f64(x), 1, "e4m3")
    wq = mxq(f64(w), 0, "e4m3")
    z = xq.transpose(0, 2, 1) @ wq
    h = np.maximum(z, 0.0) * f64(ni)
    adq = mxq(f64(ad), 1, "e4m3")
    hq = mxq(h, 1, "e4m3")
    y = adq.transpose(0, 2, 1) @ hq
    out_ = y * sigmoid(f64(og)) + f64(r)
    return out_

@@ -1,0 +1,190 @@
+from contextlib import ExitStack
+
+import concourse.mybir as mybir
+
+G, D, I, N, J = 4, 128, 128, 512, 128
+FLOPS = 2 * G * D * I * N + 2 * G * I * J * N
+
+F32 = mybir.dt.float32
+BF16 = mybir.dt.bfloat16
+U32 = mybir.dt.uint32
+U8 = mybir.dt.uint8
+FP8X4 = mybir.dt.float8_e4m3fn_x4
+ALU = mybir.AluOpType
+ACT = mybir.ActivationFunctionType
+
+P = 128
+ROWS = 32
+PACK = 4
+NB = 128
+HALF = 256
+USED = 96
+TILE_ROW = (0, 64)
+
+
+def tile_rows_gnn_gated_kernel(tc, x, w, ni, ad, og, r, out):
+    nc = tc.nc
+    with ExitStack() as ctx:
+        sb = ctx.enter_context(tc.tile_pool(name="sb", bufs=1))
+        ps = ctx.enter_context(tc.psum_pool(name="ps", bufs=1))
+        ctx.enter_context(tc.manual_schedule())
+
+        x_raw = sb.tile([P, G, PACK, I], F32, name="x_raw")
+        w_raw = sb.tile([P, PACK, HALF], F32, name="w_raw")
+        ad_raw = sb.tile([P, PACK, J], F32, name="ad_raw")
+        ni_sb = sb.tile([P, PACK], F32, name="ni_sb")
+        og_sb = sb.tile([P, 2, G, HALF], F32, name="og_sb")
+        r_sb = sb.tile([P, 2, G, HALF], F32, name="r_sb")
+        gate = sb.tile([P, 2, G, HALF], F32, name="gate")
+        prod = sb.tile([P, 2, G, HALF], F32, name="prod")
+        res = sb.tile([P, 2, G, HALF], F32, name="res")
+        warm_in = sb.tile([P, 8], F32, name="warm_in")
+        warm_out = sb.tile([P, 8], F32, name="warm_out")
+
+        x_bf = sb.tile([P, PACK, G, ROWS, PACK], BF16, name="x_bf", align_bytes=64)
+        w_bf = sb.tile([P, HALF, PACK], BF16, name="w_bf", align_bytes=64)
+        ad_bf = sb.tile([P, J, PACK], BF16, name="ad_bf", align_bytes=64)
+        h_bf = sb.tile([P, N, PACK], BF16, name="h_bf", align_bytes=64)
+        x_c = sb.tile([P, PACK, P], U32, name="x_c", align_bytes=64)
+        x_s = sb.tile([P, PACK, P], U8, name="x_s", align_bytes=64)
+        w_c = sb.tile([P, HALF], U32, name="w_c", align_bytes=64)
+        w_s = sb.tile([P, HALF], U8, name="w_s", align_bytes=64)
+        ad_c = sb.tile([P, J], U32, name="ad_c", align_bytes=64)
+        ad_s = sb.tile([P, J], U8, name="ad_s", align_bytes=64)
+        h_c = sb.tile([P, N], U32, name="h_c", align_bytes=64)
+        h_s = sb.tile([P, N], U8, name="h_s", align_bytes=64)
+
+        z_ps = [ps.tile([P, PACK, NB], F32, name="z%d" % b) for b in range(4)]
+        y_ps = [ps.tile([P, N], F32, name="y%d" % g) for g in range(G)]
+
+        x_v = x.rearrange("g (q j) i -> q g (j i)", j=PACK)
+        w_v = w.rearrange("(q j) n -> q j n", j=PACK)
+        og_v = og.rearrange("g j n -> j g n")
+        r_v = r.rearrange("g j n -> j g n")
+        out_v = out.rearrange("g j n -> j g n")
+        queues = (nc.sync, nc.scalar)
+
+        for pair in range(2):
+            for u in range(2):
+                r0 = TILE_ROW[u]
+                queues[u].dma_start(
+                    out=x_raw[r0 : r0 + ROWS, 2 * pair : 2 * pair + 2].rearrange("q g j i -> q g (j i)"),
+                    in_=x_v[:, 2 * pair : 2 * pair + 2, :],
+                )
+        for u in range(2):
+            r0 = TILE_ROW[u]
+            queues[u].dma_start(out=w_raw[r0 : r0 + ROWS], in_=w_v[:, :, u * HALF : (u + 1) * HALF])
+        nc.sync.dma_start(out=ni_sb[:], in_=ni.rearrange("g (q t) o -> (g q) (t o)", t=PACK))
+        nc.sync.dma_start(out=ad_raw[:], in_=ad.rearrange("g (q t) j -> (g q) t j", t=PACK))
+        for src, dst in ((og_v, og_sb), (r_v, r_sb)):
+            for hf in range(2):
+                nc.sync.dma_start(out=dst[:, hf], in_=src[:, :, hf * HALF : (hf + 1) * HALF])
+
+        nc.gpsimd.memset(warm_in[:], 0.0)
+        nc.scalar.activation(out=warm_out[:], in_=warm_in[:], func=ACT.Sigmoid)
+        nc.vector.memset(x_raw[ROWS : 2 * ROWS], 0.0)
+        nc.vector.memset(w_raw[ROWS : 2 * ROWS], 0.0)
+
+        def quantize(codes, scales, values):
+            nc.vector.quantize_mx(out=codes.bitcast(FP8X4), scales=scales, in_=values)
+
+        for g in range(G):
+            nc.vector.tensor_copy(
+                out=x_bf[:USED, :, g].rearrange("q t m j -> q m t j"),
+                in_=x_raw[:USED, g].rearrange("q j (m t) -> q m t j", t=PACK),
+            )
+        for s in range(2):
+            cols = slice(s * NB, (s + 1) * NB)
+            nc.scalar.copy(out=w_bf[:USED, cols], in_=w_raw[:USED, :, cols].rearrange("q j n -> q n j"))
+        nc.scalar.copy(out=ad_bf[:], in_=ad_raw[:].rearrange("q t j -> q j t"))
+        for hf in range(2):
+            nc.scalar.activation(out=gate[:, hf], in_=og_sb[:, hf], func=ACT.Sigmoid)
+
+        quantize(
+            x_c[:USED].rearrange("q t c -> q (t c)"),
+            x_s[:USED].rearrange("q t c -> q (t c)"),
+            x_bf[:USED].rearrange("q t g m j -> q (t g m j)"),
+        )
+        for s in range(2):
+            cols = slice(s * NB, (s + 1) * NB)
+            quantize(w_c[:USED, cols], w_s[:USED, cols], w_bf[:USED, cols].rearrange("q n j -> q (n j)"))
+        quantize(ad_c[:], ad_s[:], ad_bf[:].rearrange("q j t -> q (j t)"))
+
+        for s in range(2):
+            cols = slice(s * NB, (s + 1) * NB)
+            for t in range(PACK):
+                for u in range(2):
+                    rows = slice(TILE_ROW[u], TILE_ROW[u] + ROWS)
+                    nc.tensor.matmul_mx(
+                        out=z_ps[2 * u + s][:, t, :],
+                        lhsT=x_c[rows, t, :].bitcast(FP8X4),
+                        lhsT_scale=x_s[rows, t, :],
+                        rhs=w_c[rows, cols].bitcast(FP8X4),
+                        rhs_scale=w_s[rows, cols],
+                        start=True,
+                        stop=True,
+                    )
+
+        ni_b = ni_sb[:].unsqueeze(1).to_broadcast([P, NB, PACK])
+
+        def messages(b):
+            nc.vector.scalar_tensor_tensor(
+                out=h_bf[:, b * NB : (b + 1) * NB],
+                in0=z_ps[b][:].rearrange("p t n -> p n t"),
+                scalar=0.0,
+                in1=ni_b,
+                op0=ALU.max,
+                op1=ALU.mult,
+            )
+
+        def quantize_h(b):
+            cols = slice(b * NB, (b + 1) * NB)
+            quantize(h_c[:, cols], h_s[:, cols], h_bf[:, cols].rearrange("p n t -> p (n t)"))
+
+        def second(b, g):
+            cols = slice(b * NB, (b + 1) * NB)
+            rows = slice(g * ROWS, (g + 1) * ROWS)
+            nc.tensor.matmul_mx(
+                out=y_ps[g][:, cols],
+                lhsT=ad_c[rows, :].bitcast(FP8X4),
+                lhsT_scale=ad_s[rows, :],
+                rhs=h_c[rows, cols].bitcast(FP8X4),
+                rhs_scale=h_s[rows, cols],
+                start=True,
+                stop=True,
+            )
+
+        def gate_mul(hf, g):
+            nc.vector.tensor_tensor(
+                out=prod[:, hf, g], in0=y_ps[g][:, hf * HALF : (hf + 1) * HALF], in1=gate[:, hf, g], op=ALU.mult
+            )
+
+        def add_store(engine, hf, g0, g1):
+            engine.tensor_tensor(out=res[:, hf, g0:g1], in0=prod[:, hf, g0:g1], in1=r_sb[:, hf, g0:g1], op=ALU.add)
+
+        def store(hf, g0, g1):
+            nc.sync.dma_start(out=out_v[:, g0:g1, hf * HALF : (hf + 1) * HALF], in_=res[:, hf, g0:g1])
+
+        messages(0)
+        messages(1)
+        quantize_h(0)
+        messages(2)
+        quantize_h(1)
+        for b in range(2):
+            for g in range(G):
+                second(b, g)
+        messages(3)
+        quantize_h(2)
+        quantize_h(3)
+        for g in range(G):
+            gate_mul(0, g)
+            second(2, g)
+            second(3, g)
+            add_store(nc.gpsimd, 0, g, g + 1)
+            if g % 2 == 1:
+                store(0, g - 1, g + 1)
+        for g in range(G):
+            gate_mul(1, g)
+        for g0 in (0, 2):
+            add_store(nc.vector, 1, g0, g0 + 2)
+            store(1, g0, g0 + 2)

@@ -20,6 +20,7 @@ NB = 128
 HALF = 256
 USED = 96
 TILE_ROW = (0, 64)
+SPLIT = 12
 
 
 def tile_rows_gnn_gated_kernel(tc, x, w, ni, ad, og, r, out):
@@ -30,7 +31,7 @@ def tile_rows_gnn_gated_kernel(tc, x, w, ni, ad, og, r, out):
         ctx.enter_context(tc.manual_schedule())
 
         x_raw = sb.tile([P, G, PACK, I], F32, name="x_raw")
-        w_raw = sb.tile([P, PACK, HALF], F32, name="w_raw")
+        w_raw = sb.tile([P, 2, PACK, NB], F32, name="w_raw")
         ad_raw = sb.tile([P, PACK, J], F32, name="ad_raw")
         ni_sb = sb.tile([P, PACK], F32, name="ni_sb")
         og_sb = sb.tile([P, 2, G, HALF], F32, name="og_sb")
@@ -64,6 +65,15 @@ def tile_rows_gnn_gated_kernel(tc, x, w, ni, ad, og, r, out):
         out_v = out.rearrange("g j n -> j g n")
         queues = (nc.sync, nc.scalar)
 
+        def load_w(s):
+            for u in range(2):
+                r0 = TILE_ROW[u]
+                n0 = u * HALF + s * NB
+                queues[u].dma_start(out=w_raw[r0 : r0 + ROWS, s], in_=w_v[:, :, n0 : n0 + NB])
+
+        nc.gpsimd.memset(warm_in[:], 0.0)
+        nc.gpsimd.dma_start(out=ni_sb[:], in_=ni.rearrange("g (q t) o -> (g q) (t o)", t=PACK))
+        load_w(0)
         for pair in range(2):
             for u in range(2):
                 r0 = TILE_ROW[u]
@@ -71,59 +81,67 @@ def tile_rows_gnn_gated_kernel(tc, x, w, ni, ad, og, r, out):
                     out=x_raw[r0 : r0 + ROWS, 2 * pair : 2 * pair + 2].rearrange("q g j i -> q g (j i)"),
                     in_=x_v[:, 2 * pair : 2 * pair + 2, :],
                 )
-        for u in range(2):
-            r0 = TILE_ROW[u]
-            queues[u].dma_start(out=w_raw[r0 : r0 + ROWS], in_=w_v[:, :, u * HALF : (u + 1) * HALF])
-        nc.sync.dma_start(out=ni_sb[:], in_=ni.rearrange("g (q t) o -> (g q) (t o)", t=PACK))
+        load_w(1)
         nc.sync.dma_start(out=ad_raw[:], in_=ad.rearrange("g (q t) j -> (g q) t j", t=PACK))
         for src, dst in ((og_v, og_sb), (r_v, r_sb)):
             for hf in range(2):
                 nc.sync.dma_start(out=dst[:, hf], in_=src[:, :, hf * HALF : (hf + 1) * HALF])
 
-        nc.gpsimd.memset(warm_in[:], 0.0)
         nc.scalar.activation(out=warm_out[:], in_=warm_in[:], func=ACT.Sigmoid)
-        nc.vector.memset(x_raw[ROWS : 2 * ROWS], 0.0)
         nc.vector.memset(w_raw[ROWS : 2 * ROWS], 0.0)
+        nc.vector.memset(x_raw[ROWS : 2 * ROWS], 0.0)
 
         def quantize(codes, scales, values):
             nc.vector.quantize_mx(out=codes.bitcast(FP8X4), scales=scales, in_=values)
 
-        for g in range(G):
-            nc.vector.tensor_copy(
-                out=x_bf[:USED, :, g].rearrange("q t m j -> q m t j"),
-                in_=x_raw[:USED, g].rearrange("q j (m t) -> q m t j", t=PACK),
+        def group_x(copy, g, m0, m1):
+            copy(
+                out=x_bf[:USED, :, g, m0:m1].rearrange("q t m j -> q m t j"),
+                in_=x_raw[:USED, g, :, PACK * m0 : PACK * m1].rearrange("q j (m t) -> q m t j", t=PACK),
             )
-        for s in range(2):
+
+        def group_w(copy, s):
+            copy(out=w_bf[:USED, s * NB : (s + 1) * NB], in_=w_raw[:USED, s].rearrange("q j n -> q n j"))
+
+        def quantize_w(s):
             cols = slice(s * NB, (s + 1) * NB)
-            nc.scalar.copy(out=w_bf[:USED, cols], in_=w_raw[:USED, :, cols].rearrange("q j n -> q n j"))
+            quantize(w_c[:USED, cols], w_s[:USED, cols], w_bf[:USED, cols].rearrange("q n j -> q (n j)"))
+
+        def first(b, t):
+            u, s = divmod(b, 2)
+            cols = slice(s * NB, (s + 1) * NB)
+            rows = slice(TILE_ROW[u], TILE_ROW[u] + ROWS)
+            nc.tensor.matmul_mx(
+                out=z_ps[b][:, t, :],
+                lhsT=x_c[rows, t, :].bitcast(FP8X4),
+                lhsT_scale=x_s[rows, t, :],
+                rhs=w_c[rows, cols].bitcast(FP8X4),
+                rhs_scale=w_s[rows, cols],
+                start=True,
+                stop=True,
+            )
+
+        group_w(nc.vector.tensor_copy, 0)
+        group_x(nc.vector.tensor_copy, 0, 0, ROWS)
+        quantize_w(0)
+        group_x(nc.vector.tensor_copy, 1, 0, ROWS)
+        group_x(nc.vector.tensor_copy, 2, 0, ROWS)
+        group_x(nc.vector.tensor_copy, 3, 0, SPLIT)
+        group_x(nc.scalar.copy, 3, SPLIT, ROWS)
+        group_w(nc.scalar.copy, 1)
         nc.scalar.copy(out=ad_bf[:], in_=ad_raw[:].rearrange("q t j -> q j t"))
         for hf in range(2):
             nc.scalar.activation(out=gate[:, hf], in_=og_sb[:, hf], func=ACT.Sigmoid)
 
-        quantize(
-            x_c[:USED].rearrange("q t c -> q (t c)"),
-            x_s[:USED].rearrange("q t c -> q (t c)"),
-            x_bf[:USED].rearrange("q t g m j -> q (t g m j)"),
-        )
-        for s in range(2):
-            cols = slice(s * NB, (s + 1) * NB)
-            quantize(w_c[:USED, cols], w_s[:USED, cols], w_bf[:USED, cols].rearrange("q n j -> q (n j)"))
-        quantize(ad_c[:], ad_s[:], ad_bf[:].rearrange("q j t -> q (j t)"))
-
-        for s in range(2):
-            cols = slice(s * NB, (s + 1) * NB)
-            for t in range(PACK):
-                for u in range(2):
-                    rows = slice(TILE_ROW[u], TILE_ROW[u] + ROWS)
-                    nc.tensor.matmul_mx(
-                        out=z_ps[2 * u + s][:, t, :],
-                        lhsT=x_c[rows, t, :].bitcast(FP8X4),
-                        lhsT_scale=x_s[rows, t, :],
-                        rhs=w_c[rows, cols].bitcast(FP8X4),
-                        rhs_scale=w_s[rows, cols],
-                        start=True,
-                        stop=True,
-                    )
+        for t in range(PACK):
+            quantize(x_c[:USED, t], x_s[:USED, t], x_bf[:USED, t].rearrange("q g m j -> q (g m j)"))
+            first(0, t)
+        quantize_w(1)
+        for t in range(PACK):
+            first(1, t)
+            first(2, t)
+        for t in range(PACK):
+            first(3, t)
 
         ni_b = ni_sb[:].unsqueeze(1).to_broadcast([P, NB, PACK])
 
@@ -166,13 +184,15 @@ def tile_rows_gnn_gated_kernel(tc, x, w, ni, ad, og, r, out):
             nc.sync.dma_start(out=out_v[:, g0:g1, hf * HALF : (hf + 1) * HALF], in_=res[:, hf, g0:g1])
 
         messages(0)
+        quantize(ad_c[:], ad_s[:], ad_bf[:].rearrange("q j t -> q (j t)"))
         messages(1)
         quantize_h(0)
+        for g in range(G):
+            second(0, g)
         messages(2)
         quantize_h(1)
-        for b in range(2):
-            for g in range(G):
-                second(b, g)
+        for g in range(G):
+            second(1, g)
         messages(3)
         quantize_h(2)
         quantize_h(3)
@@ -180,11 +200,13 @@ def tile_rows_gnn_gated_kernel(tc, x, w, ni, ad, og, r, out):
             gate_mul(0, g)
             second(2, g)
             second(3, g)
-            add_store(nc.gpsimd, 0, g, g + 1)
-            if g % 2 == 1:
-                store(0, g - 1, g + 1)
+            if g < 3:
+                add_store(nc.gpsimd, 0, g, g + 1)
+        store(0, 0, 2)
         for g in range(G):
             gate_mul(1, g)
-        for g0 in (0, 2):
-            add_store(nc.vector, 1, g0, g0 + 2)
-            store(1, g0, g0 + 2)
+        add_store(nc.vector, 0, 3, 4)
+        store(0, 2, 4)
+        for g0, g1 in ((0, 2), (2, 3), (3, 4)):
+            add_store(nc.vector, 1, g0, g1)
+            store(1, g0, g1)

@@ -18,9 +18,6 @@ ROWS = 32
 PACK = 4
 NB = 128
 HALF = 256
-USED = 96
-TILE_ROW = (0, 64)
-SPLIT = 12
 
 
 def tile_rows_gnn_gated_kernel(tc, x, w, ni, ad, og, r, out):
@@ -30,8 +27,8 @@ def tile_rows_gnn_gated_kernel(tc, x, w, ni, ad, og, r, out):
         ps = ctx.enter_context(tc.psum_pool(name="ps", bufs=1))
         ctx.enter_context(tc.manual_schedule())
 
-        x_raw = sb.tile([P, G, PACK, I], F32, name="x_raw")
-        w_raw = sb.tile([P, 2, PACK, NB], F32, name="w_raw")
+        x_raw = sb.tile([ROWS, G, PACK, I], F32, name="x_raw")
+        w_raw = sb.tile([ROWS, PACK, N], F32, name="w_raw")
         ad_raw = sb.tile([P, PACK, J], F32, name="ad_raw")
         ni_sb = sb.tile([P, PACK], F32, name="ni_sb")
         og_sb = sb.tile([P, 2, G, HALF], F32, name="og_sb")
@@ -42,14 +39,14 @@ def tile_rows_gnn_gated_kernel(tc, x, w, ni, ad, og, r, out):
         warm_in = sb.tile([P, 8], F32, name="warm_in")
         warm_out = sb.tile([P, 8], F32, name="warm_out")
 
-        x_bf = sb.tile([P, PACK, G, ROWS, PACK], BF16, name="x_bf", align_bytes=64)
-        w_bf = sb.tile([P, HALF, PACK], BF16, name="w_bf", align_bytes=64)
+        x_bf = sb.tile([ROWS, PACK, G, ROWS, PACK], BF16, name="x_bf", align_bytes=64)
+        w_bf = sb.tile([ROWS, N, PACK], BF16, name="w_bf", align_bytes=64)
         ad_bf = sb.tile([P, J, PACK], BF16, name="ad_bf", align_bytes=64)
         h_bf = sb.tile([P, N, PACK], BF16, name="h_bf", align_bytes=64)
-        x_c = sb.tile([P, PACK, P], U32, name="x_c", align_bytes=64)
-        x_s = sb.tile([P, PACK, P], U8, name="x_s", align_bytes=64)
-        w_c = sb.tile([P, HALF], U32, name="w_c", align_bytes=64)
-        w_s = sb.tile([P, HALF], U8, name="w_s", align_bytes=64)
+        x_c = sb.tile([ROWS, PACK, P], U32, name="x_c", align_bytes=64)
+        x_s = sb.tile([ROWS, PACK, P], U8, name="x_s", align_bytes=64)
+        w_c = sb.tile([ROWS, N], U32, name="w_c", align_bytes=64)
+        w_s = sb.tile([ROWS, N], U8, name="w_s", align_bytes=64)
         ad_c = sb.tile([P, J], U32, name="ad_c", align_bytes=64)
         ad_s = sb.tile([P, J], U8, name="ad_s", align_bytes=64)
         h_c = sb.tile([P, N], U32, name="h_c", align_bytes=64)
@@ -63,85 +60,86 @@ def tile_rows_gnn_gated_kernel(tc, x, w, ni, ad, og, r, out):
         og_v = og.rearrange("g j n -> j g n")
         r_v = r.rearrange("g j n -> j g n")
         out_v = out.rearrange("g j n -> j g n")
-        queues = (nc.sync, nc.scalar)
 
-        def load_w(s):
-            for u in range(2):
-                r0 = TILE_ROW[u]
-                n0 = u * HALF + s * NB
-                queues[u].dma_start(out=w_raw[r0 : r0 + ROWS, s], in_=w_v[:, :, n0 : n0 + NB])
+        def load_w(b0, b1):
+            nc.sync.dma_start(out=w_raw[:, :, b0 * NB : b1 * NB], in_=w_v[:, :, b0 * NB : b1 * NB])
 
         nc.gpsimd.memset(warm_in[:], 0.0)
-        nc.gpsimd.dma_start(out=ni_sb[:], in_=ni.rearrange("g (q t) o -> (g q) (t o)", t=PACK))
-        load_w(0)
+        nc.scalar.dma_start(out=ni_sb[:], in_=ni.rearrange("g (q t) o -> (g q) (t o)", t=PACK))
+        load_w(0, 1)
         for pair in range(2):
-            for u in range(2):
-                r0 = TILE_ROW[u]
-                queues[u].dma_start(
-                    out=x_raw[r0 : r0 + ROWS, 2 * pair : 2 * pair + 2].rearrange("q g j i -> q g (j i)"),
-                    in_=x_v[:, 2 * pair : 2 * pair + 2, :],
-                )
-        load_w(1)
+            nc.sync.dma_start(
+                out=x_raw[:, 2 * pair : 2 * pair + 2].rearrange("q g j i -> q g (j i)"),
+                in_=x_v[:, 2 * pair : 2 * pair + 2, :],
+            )
+        load_w(1, 2)
+        load_w(2, 4)
         nc.sync.dma_start(out=ad_raw[:], in_=ad.rearrange("g (q t) j -> (g q) t j", t=PACK))
-        for src, dst in ((og_v, og_sb), (r_v, r_sb)):
-            for hf in range(2):
-                nc.sync.dma_start(out=dst[:, hf], in_=src[:, :, hf * HALF : (hf + 1) * HALF])
+        for src, dst, hf, g0, g1 in (
+            (og_v, og_sb, 0, 0, 4),
+            (r_v, r_sb, 0, 0, 2),
+            (og_v, og_sb, 1, 0, 4),
+            (r_v, r_sb, 0, 2, 4),
+            (r_v, r_sb, 1, 0, 4),
+        ):
+            nc.sync.dma_start(out=dst[:, hf, g0:g1], in_=src[:, g0:g1, hf * HALF : (hf + 1) * HALF])
 
         nc.scalar.activation(out=warm_out[:], in_=warm_in[:], func=ACT.Sigmoid)
-        nc.vector.memset(w_raw[ROWS : 2 * ROWS], 0.0)
-        nc.vector.memset(x_raw[ROWS : 2 * ROWS], 0.0)
 
         def quantize(codes, scales, values):
             nc.vector.quantize_mx(out=codes.bitcast(FP8X4), scales=scales, in_=values)
 
-        def group_x(copy, g, m0, m1):
+        def group_x(copy, g, t0, t1):
             copy(
-                out=x_bf[:USED, :, g, m0:m1].rearrange("q t m j -> q m t j"),
-                in_=x_raw[:USED, g, :, PACK * m0 : PACK * m1].rearrange("q j (m t) -> q m t j", t=PACK),
+                out=x_bf[:, t0:t1, g].rearrange("q t m j -> q m t j"),
+                in_=x_raw[:, g].rearrange("q j (m t) -> q m t j", t=PACK)[:, :, t0:t1, :],
             )
 
-        def group_w(copy, s):
-            copy(out=w_bf[:USED, s * NB : (s + 1) * NB], in_=w_raw[:USED, s].rearrange("q j n -> q n j"))
+        def group_w(copy, b):
+            cols = slice(b * NB, (b + 1) * NB)
+            copy(out=w_bf[:, cols], in_=w_raw[:, :, cols].rearrange("q j n -> q n j"))
 
-        def quantize_w(s):
-            cols = slice(s * NB, (s + 1) * NB)
-            quantize(w_c[:USED, cols], w_s[:USED, cols], w_bf[:USED, cols].rearrange("q n j -> q (n j)"))
+        def quantize_w(b):
+            cols = slice(b * NB, (b + 1) * NB)
+            quantize(w_c[:, cols], w_s[:, cols], w_bf[:, cols].rearrange("q n j -> q (n j)"))
 
         def first(b, t):
-            u, s = divmod(b, 2)
-            cols = slice(s * NB, (s + 1) * NB)
-            rows = slice(TILE_ROW[u], TILE_ROW[u] + ROWS)
+            cols = slice(b * NB, (b + 1) * NB)
             nc.tensor.matmul_mx(
                 out=z_ps[b][:, t, :],
-                lhsT=x_c[rows, t, :].bitcast(FP8X4),
-                lhsT_scale=x_s[rows, t, :],
-                rhs=w_c[rows, cols].bitcast(FP8X4),
-                rhs_scale=w_s[rows, cols],
+                lhsT=x_c[:, t, :].bitcast(FP8X4),
+                lhsT_scale=x_s[:, t, :],
+                rhs=w_c[:, cols].bitcast(FP8X4),
+                rhs_scale=w_s[:, cols],
                 start=True,
                 stop=True,
             )
 
+        def first_block(b):
+            quantize_w(b)
+            for t in range(PACK):
+                first(b, t)
+
         group_w(nc.vector.tensor_copy, 0)
-        group_x(nc.vector.tensor_copy, 0, 0, ROWS)
+        group_x(nc.vector.tensor_copy, 0, 0, 4)
         quantize_w(0)
-        group_x(nc.vector.tensor_copy, 1, 0, ROWS)
-        group_x(nc.vector.tensor_copy, 2, 0, ROWS)
-        group_x(nc.vector.tensor_copy, 3, 0, SPLIT)
-        group_x(nc.scalar.copy, 3, SPLIT, ROWS)
+        for g in (1, 2, 3):
+            group_x(nc.vector.tensor_copy, g, 0, 2)
+        group_x(nc.vector.tensor_copy, 2, 2, 4)
+        group_x(nc.scalar.copy, 1, 2, 4)
+        group_x(nc.scalar.copy, 3, 2, 4)
         group_w(nc.scalar.copy, 1)
+        group_w(nc.scalar.copy, 2)
         nc.scalar.copy(out=ad_bf[:], in_=ad_raw[:].rearrange("q t j -> q j t"))
+        group_w(nc.scalar.copy, 3)
         for hf in range(2):
-            nc.scalar.activation(out=gate[:, hf], in_=og_sb[:, hf], func=ACT.Sigmoid)
+            for graphs in (slice(1, 3), slice(0, 4, 3)):
+                nc.scalar.activation(out=gate[:, hf, graphs], in_=og_sb[:, hf, graphs], func=ACT.Sigmoid)
 
         for t in range(PACK):
-            quantize(x_c[:USED, t], x_s[:USED, t], x_bf[:USED, t].rearrange("q g m j -> q (g m j)"))
+            quantize(x_c[:, t], x_s[:, t], x_bf[:, t].rearrange("q g m j -> q (g m j)"))
             first(0, t)
-        quantize_w(1)
-        for t in range(PACK):
-            first(1, t)
-            first(2, t)
-        for t in range(PACK):
-            first(3, t)
+        first_block(1)
 
         ni_b = ni_sb[:].unsqueeze(1).to_broadcast([P, NB, PACK])
 
@@ -177,36 +175,38 @@ def tile_rows_gnn_gated_kernel(tc, x, w, ni, ad, og, r, out):
                 out=prod[:, hf, g], in0=y_ps[g][:, hf * HALF : (hf + 1) * HALF], in1=gate[:, hf, g], op=ALU.mult
             )
 
-        def add_store(engine, hf, g0, g1):
-            engine.tensor_tensor(out=res[:, hf, g0:g1], in0=prod[:, hf, g0:g1], in1=r_sb[:, hf, g0:g1], op=ALU.add)
-
-        def store(hf, g0, g1):
-            nc.sync.dma_start(out=out_v[:, g0:g1, hf * HALF : (hf + 1) * HALF], in_=res[:, hf, g0:g1])
+        def add_store(engine, hf, g):
+            engine.tensor_tensor(out=res[:, hf, g], in0=prod[:, hf, g], in1=r_sb[:, hf, g], op=ALU.add)
+            nc.sync.dma_start(out=out_v[:, g, hf * HALF : (hf + 1) * HALF], in_=res[:, hf, g])
 
         messages(0)
-        quantize(ad_c[:], ad_s[:], ad_bf[:].rearrange("q j t -> q (j t)"))
+        first_block(2)
         messages(1)
         quantize_h(0)
-        for g in range(G):
-            second(0, g)
-        messages(2)
+        quantize(ad_c[:], ad_s[:], ad_bf[:].rearrange("q j t -> q (j t)"))
         quantize_h(1)
-        for g in range(G):
-            second(1, g)
+        for b in (0, 1):
+            for g in (1, 2, 3):
+                second(b, g)
+        first_block(3)
+        second(0, 0)
+        second(1, 0)
+        messages(2)
+        gate_mul(0, 1)
+        add_store(nc.gpsimd, 0, 1)
+        gate_mul(0, 2)
         messages(3)
-        quantize_h(2)
-        quantize_h(3)
-        for g in range(G):
+        for b in (2, 3):
+            quantize_h(b)
+            second(b, 1)
+            second(b, 2)
+        for g in (0, 3):
             gate_mul(0, g)
             second(2, g)
             second(3, g)
-            if g < 3:
-                add_store(nc.gpsimd, 0, g, g + 1)
-        store(0, 0, 2)
-        for g in range(G):
+            add_store(nc.gpsimd, 0, g)
+        for g in (1, 2, 0, 3):
             gate_mul(1, g)
-        add_store(nc.vector, 0, 3, 4)
-        store(0, 2, 4)
-        for g0, g1 in ((0, 2), (2, 3), (3, 4)):
-            add_store(nc.vector, 1, g0, g1)
-            store(1, g0, g1)
+        add_store(nc.vector, 0, 2)
+        for g in (1, 2, 0, 3):
+            add_store(nc.vector, 1, g)

from contextlib import ExitStack

import concourse.mybir as mybir

G, D, I, N, J = 4, 128, 128, 512, 128
FLOPS = 2 * G * D * I * N + 2 * G * I * J * N

F32 = mybir.dt.float32
BF16 = mybir.dt.bfloat16
U32 = mybir.dt.uint32
U8 = mybir.dt.uint8
FP8X4 = mybir.dt.float8_e4m3fn_x4
ALU = mybir.AluOpType
ACT = mybir.ActivationFunctionType

P = 128
ROWS = 32
PACK = 4
NB = 128
HALF = 256


def tile_rows_gnn_gated_kernel(tc, x, w, ni, ad, og, r, out):
    nc = tc.nc
    with ExitStack() as ctx:
        sb = ctx.enter_context(tc.tile_pool(name="sb", bufs=1))
        ps = ctx.enter_context(tc.psum_pool(name="ps", bufs=1))
        ctx.enter_context(tc.manual_schedule())

        x_raw = sb.tile([ROWS, G, PACK, I], F32, name="x_raw")
        w_raw = sb.tile([ROWS, PACK, N], F32, name="w_raw")
        ad_raw = sb.tile([P, PACK, J], F32, name="ad_raw")
        ni_sb = sb.tile([P, PACK], F32, name="ni_sb")
        og_sb = sb.tile([P, 2, G, HALF], F32, name="og_sb")
        r_sb = sb.tile([P, 2, G, HALF], F32, name="r_sb")
        gate = sb.tile([P, 2, G, HALF], F32, name="gate")
        prod = sb.tile([P, 2, G, HALF], F32, name="prod")
        res = sb.tile([P, 2, G, HALF], F32, name="res")
        warm_in = sb.tile([P, 8], F32, name="warm_in")
        warm_out = sb.tile([P, 8], F32, name="warm_out")

        x_bf = sb.tile([ROWS, PACK, G, ROWS, PACK], BF16, name="x_bf", align_bytes=64)
        w_bf = sb.tile([ROWS, N, PACK], BF16, name="w_bf", align_bytes=64)
        ad_bf = sb.tile([P, J, PACK], BF16, name="ad_bf", align_bytes=64)
        h_bf = sb.tile([P, N, PACK], BF16, name="h_bf", align_bytes=64)
        x_c = sb.tile([ROWS, PACK, P], U32, name="x_c", align_bytes=64)
        x_s = sb.tile([ROWS, PACK, P], U8, name="x_s", align_bytes=64)
        w_c = sb.tile([ROWS, N], U32, name="w_c", align_bytes=64)
        w_s = sb.tile([ROWS, N], U8, name="w_s", align_bytes=64)
        ad_c = sb.tile([P, J], U32, name="ad_c", align_bytes=64)
        ad_s = sb.tile([P, J], U8, name="ad_s", align_bytes=64)
        h_c = sb.tile([P, N], U32, name="h_c", align_bytes=64)
        h_s = sb.tile([P, N], U8, name="h_s", align_bytes=64)

        z_ps = [ps.tile([P, PACK, NB], F32, name="z%d" % b) for b in range(4)]
        y_ps = [ps.tile([P, N], F32, name="y%d" % g) for g in range(G)]

        x_v = x.rearrange("g (q j) i -> q g (j i)", j=PACK)
        w_v = w.rearrange("(q j) n -> q j n", j=PACK)
        og_v = og.rearrange("g j n -> j g n")
        r_v = r.rearrange("g j n -> j g n")
        out_v = out.rearrange("g j n -> j g n")

        def load_w(b0, b1):
            nc.sync.dma_start(out=w_raw[:, :, b0 * NB : b1 * NB], in_=w_v[:, :, b0 * NB : b1 * NB])

        nc.gpsimd.memset(warm_in[:], 0.0)
        nc.scalar.dma_start(out=ni_sb[:], in_=ni.rearrange("g (q t) o -> (g q) (t o)", t=PACK))
        load_w(0, 1)
        for pair in range(2):
            nc.sync.dma_start(
                out=x_raw[:, 2 * pair : 2 * pair + 2].rearrange("q g j i -> q g (j i)"),
                in_=x_v[:, 2 * pair : 2 * pair + 2, :],
            )
        load_w(1, 2)
        load_w(2, 4)
        nc.sync.dma_start(out=ad_raw[:], in_=ad.rearrange("g (q t) j -> (g q) t j", t=PACK))
        for src, dst, hf, g0, g1 in (
            (og_v, og_sb, 0, 0, 4),
            (r_v, r_sb, 0, 0, 2),
            (og_v, og_sb, 1, 0, 4),
            (r_v, r_sb, 0, 2, 4),
            (r_v, r_sb, 1, 0, 4),
        ):
            nc.sync.dma_start(out=dst[:, hf, g0:g1], in_=src[:, g0:g1, hf * HALF : (hf + 1) * HALF])

        nc.scalar.activation(out=warm_out[:], in_=warm_in[:], func=ACT.Sigmoid)

        def quantize(codes, scales, values):
            nc.vector.quantize_mx(out=codes.bitcast(FP8X4), scales=scales, in_=values)

        def group_x(copy, g, t0, t1):
            copy(
                out=x_bf[:, t0:t1, g].rearrange("q t m j -> q m t j"),
                in_=x_raw[:, g].rearrange("q j (m t) -> q m t j", t=PACK)[:, :, t0:t1, :],
            )

        def group_w(copy, b):
            cols = slice(b * NB, (b + 1) * NB)
            copy(out=w_bf[:, cols], in_=w_raw[:, :, cols].rearrange("q j n -> q n j"))

        def quantize_w(b):
            cols = slice(b * NB, (b + 1) * NB)
            quantize(w_c[:, cols], w_s[:, cols], w_bf[:, cols].rearrange("q n j -> q (n j)"))

        def first(b, t):
            cols = slice(b * NB, (b + 1) * NB)
            nc.tensor.matmul_mx(
                out=z_ps[b][:, t, :],
                lhsT=x_c[:, t, :].bitcast(FP8X4),
                lhsT_scale=x_s[:, t, :],
                rhs=w_c[:, cols].bitcast(FP8X4),
                rhs_scale=w_s[:, cols],
                start=True,
                stop=True,
            )

        def first_block(b):
            quantize_w(b)
            for t in range(PACK):
                first(b, t)

        group_w(nc.vector.tensor_copy, 0)
        group_x(nc.vector.tensor_copy, 0, 0, 4)
        quantize_w(0)
        for g in (1, 2, 3):
            group_x(nc.vector.tensor_copy, g, 0, 2)
        group_x(nc.vector.tensor_copy, 2, 2, 4)
        group_x(nc.scalar.copy, 1, 2, 4)
        group_x(nc.scalar.copy, 3, 2, 4)
        group_w(nc.scalar.copy, 1)
        group_w(nc.scalar.copy, 2)
        nc.scalar.copy(out=ad_bf[:], in_=ad_raw[:].rearrange("q t j -> q j t"))
        group_w(nc.scalar.copy, 3)
        for hf in range(2):
            for graphs in (slice(1, 3), slice(0, 4, 3)):
                nc.scalar.activation(out=gate[:, hf, graphs], in_=og_sb[:, hf, graphs], func=ACT.Sigmoid)

        for t in range(PACK):
            quantize(x_c[:, t], x_s[:, t], x_bf[:, t].rearrange("q g m j -> q (g m j)"))
            first(0, t)
        first_block(1)

        ni_b = ni_sb[:].unsqueeze(1).to_broadcast([P, NB, PACK])

        def messages(b):
            nc.vector.scalar_tensor_tensor(
                out=h_bf[:, b * NB : (b + 1) * NB],
                in0=z_ps[b][:].rearrange("p t n -> p n t"),
                scalar=0.0,
                in1=ni_b,
                op0=ALU.max,
                op1=ALU.mult,
            )

        def quantize_h(b):
            cols = slice(b * NB, (b + 1) * NB)
            quantize(h_c[:, cols], h_s[:, cols], h_bf[:, cols].rearrange("p n t -> p (n t)"))

        def second(b, g):
            cols = slice(b * NB, (b + 1) * NB)
            rows = slice(g * ROWS, (g + 1) * ROWS)
            nc.tensor.matmul_mx(
                out=y_ps[g][:, cols],
                lhsT=ad_c[rows, :].bitcast(FP8X4),
                lhsT_scale=ad_s[rows, :],
                rhs=h_c[rows, cols].bitcast(FP8X4),
                rhs_scale=h_s[rows, cols],
                start=True,
                stop=True,
            )

        def gate_mul(hf, g):
            nc.vector.tensor_tensor(
                out=prod[:, hf, g], in0=y_ps[g][:, hf * HALF : (hf + 1) * HALF], in1=gate[:, hf, g], op=ALU.mult
            )

        def add_store(engine, hf, g):
            engine.tensor_tensor(out=res[:, hf, g], in0=prod[:, hf, g], in1=r_sb[:, hf, g], op=ALU.add)
            nc.sync.dma_start(out=out_v[:, g, hf * HALF : (hf + 1) * HALF], in_=res[:, hf, g])

        messages(0)
        first_block(2)
        messages(1)
        quantize_h(0)
        quantize(ad_c[:], ad_s[:], ad_bf[:].rearrange("q j t -> q (j t)"))
        quantize_h(1)
        for b in (0, 1):
            for g in (1, 2, 3):
                second(b, g)
        first_block(3)
        second(0, 0)
        second(1, 0)
        messages(2)
        gate_mul(0, 1)
        add_store(nc.gpsimd, 0, 1)
        gate_mul(0, 2)
        messages(3)
        for b in (2, 3):
            quantize_h(b)
            second(b, 1)
            second(b, 2)
        for g in (0, 3):
            gate_mul(0, g)
            second(2, g)
            second(3, g)
            add_store(nc.gpsimd, 0, g)
        for g in (1, 2, 0, 3):
            gate_mul(1, g)
        add_store(nc.vector, 0, 2)
        for g in (1, 2, 0, 3):
            add_store(nc.vector, 1, g)
